import numpy as np
import ml_dtypes

BF16 = ml_dtypes.bfloat16


def bf(x):
    return np.asarray(x, np.float32).astype(BF16)


def f32(x):
    return np.asarray(x, np.float32)


def f64(x):
    return np.asarray(x).astype(np.float64)


def striped(idx):
    return np.tile(idx.reshape(-1, 16).T, (8, 1))


S, K, H, M, N, D, V = 256, 256, 128, 128, 512, 4, 128


def setup_inputs():
    return {"x": bf(np.random.standard_normal((K, S))), "w": bf(np.random.standard_normal((K, H)) / np.sqrt(K)), "b": f32(0.5 * np.random.standard_normal((H, 1))), "w2": bf(np.random.standard_normal((H, M)) / np.sqrt(D * H)), "offs": striped(np.random.permutation(np.tile(np.arange(S), 2))[:N])}


def reference(x, w, b, w2, offs):
    idx = offs[:16].T.reshape(-1)
    t = np.tanh(f64(w).T @ f64(x) + f64(b))
    return f64(w2).T @ sum(t[:, idx[i * V : (i + 1) * V]] for i in range(D))

@@ -1,0 +1,47 @@
+import concourse.mybir as mybir
+
+P = 128
+S, K, H, M = 256, 256, 128, 128
+D, V = 4, 128
+K_BLOCKS = K // P
+OFFSETS_PER_COLUMN = 16
+PIECE_COLUMNS = V // OFFSETS_PER_COLUMN
+
+FLOPS = 2 * K * H * S + 2 * H * M * D * V
+
+BF16, F32, U16 = mybir.dt.bfloat16, mybir.dt.float32, mybir.dt.uint16
+TANH = mybir.ActivationFunctionType.Tanh
+
+
+def tile_rows_gcn2_tanh_sum_kernel(tc, x, w, b, w2, offs, out):
+    nc = tc.nc
+    with (
+        tc.tile_pool(name="sbuf", bufs=1) as sbuf,
+        tc.psum_pool(name="psum", bufs=1) as psum,
+    ):
+        x_sb = sbuf.tile([P, K_BLOCKS, S], BF16)
+        w_sb = sbuf.tile([P, K_BLOCKS, H], BF16)
+        b_sb = sbuf.tile([H, 1], F32)
+        w2_sb = sbuf.tile([H, M], BF16)
+        offsets = sbuf.tile([P, D * PIECE_COLUMNS], U16)
+
+        nc.sync.dma_start(x_sb[:], x.rearrange("(p a) s -> p a s", a=K_BLOCKS))
+        nc.scalar.dma_start(w_sb[:], w.rearrange("(p a) h -> p a h", a=K_BLOCKS))
+        nc.scalar.dma_start(b_sb[:], b)
+        nc.sync.dma_start(w2_sb[:], w2)
+        nc.sync.dma_start(offsets[:], offs)
+
+        pre = psum.tile([H, S], F32)
+        for a in range(K_BLOCKS):
+            nc.tensor.matmul(pre[:], w_sb[:, a, :], x_sb[:, a, :], start=(a == 0), stop=(a == K_BLOCKS - 1))
+        h = sbuf.tile([H, S], BF16)
+        nc.scalar.activation(h[:], pre[:], TANH, bias=b_sb[:])
+
+        acc = psum.tile([M, V], F32)
+        for t in range(D):
+            piece = offsets[:, t * PIECE_COLUMNS : (t + 1) * PIECE_COLUMNS]
+            nc.tensor.matmul(acc[:], w2_sb[:], h[:].indirect(piece), start=(t == 0), stop=(t == D - 1))
+
+        out_sb = sbuf.tile([M, V], F32)
+        nc.vector.tensor_copy(out_sb[:], acc[:])
+        nc.sync.dma_start(out, out_sb[:])

@@ -31,6 +31,11 @@ def tile_rows_gcn2_tanh_sum_kernel(tc, x, w, b, w2, offs, out):
         nc.sync.dma_start(w2_sb[:], w2)
         nc.sync.dma_start(offsets[:], offs)
 
+        warm_in = sbuf.tile([P, 1], F32)
+        warm_out = sbuf.tile([P, 1], F32)
+        nc.vector.memset(warm_in[:], 0.0)
+        nc.scalar.activation(warm_out[:], warm_in[:], TANH)
+
         pre = psum.tile([H, S], F32)
         for a in range(K_BLOCKS):
             nc.tensor.matmul(pre[:], w_sb[:, a, :], x_sb[:, a, :], start=(a == 0), stop=(a == K_BLOCKS - 1))

@@ -4,6 +4,8 @@ P = 128
 S, K, H, M = 256, 256, 128, 128
 D, V = 4, 128
 K_BLOCKS = K // P
+NODE_HALVES = 2
+HALF = S // NODE_HALVES
 OFFSETS_PER_COLUMN = 16
 PIECE_COLUMNS = V // OFFSETS_PER_COLUMN
 
@@ -27,7 +29,7 @@ def tile_rows_gcn2_tanh_sum_kernel(tc, x, w, b, w2, offs, out):
 
         nc.sync.dma_start(x_sb[:], x.rearrange("(p a) s -> p a s", a=K_BLOCKS))
         nc.scalar.dma_start(w_sb[:], w.rearrange("(p a) h -> p a h", a=K_BLOCKS))
-        nc.scalar.dma_start(b_sb[:], b)
+        nc.sync.dma_start(b_sb[:], b)
         nc.sync.dma_start(w2_sb[:], w2)
         nc.sync.dma_start(offsets[:], offs)
 
@@ -36,11 +38,13 @@ def tile_rows_gcn2_tanh_sum_kernel(tc, x, w, b, w2, offs, out):
         nc.vector.memset(warm_in[:], 0.0)
         nc.scalar.activation(warm_out[:], warm_in[:], TANH)
 
-        pre = psum.tile([H, S], F32)
-        for a in range(K_BLOCKS):
-            nc.tensor.matmul(pre[:], w_sb[:, a, :], x_sb[:, a, :], start=(a == 0), stop=(a == K_BLOCKS - 1))
         h = sbuf.tile([H, S], BF16)
-        nc.scalar.activation(h[:], pre[:], TANH, bias=b_sb[:])
+        for half in range(NODE_HALVES):
+            nodes = slice(half * HALF, (half + 1) * HALF)
+            pre = psum.tile([H, HALF], F32, name=f"pre{half}")
+            for a in range(K_BLOCKS):
+                nc.tensor.matmul(pre[:], w_sb[:, a, :], x_sb[:, a, nodes], start=(a == 0), stop=(a == K_BLOCKS - 1))
+            nc.scalar.activation(h[:, nodes], pre[:], TANH, bias=b_sb[:])
 
         acc = psum.tile([M, V], F32)
         for t in range(D):

@@ -29,7 +29,7 @@ def tile_rows_gcn2_tanh_sum_kernel(tc, x, w, b, w2, offs, out):
 
         nc.sync.dma_start(x_sb[:], x.rearrange("(p a) s -> p a s", a=K_BLOCKS))
         nc.scalar.dma_start(w_sb[:], w.rearrange("(p a) h -> p a h", a=K_BLOCKS))
-        nc.sync.dma_start(b_sb[:], b)
+        nc.scalar.dma_start(b_sb[:], b)
         nc.sync.dma_start(w2_sb[:], w2)
         nc.sync.dma_start(offsets[:], offs)
 

import concourse.mybir as mybir

P = 128
S, K, H, M = 256, 256, 128, 128
D, V = 4, 128
K_BLOCKS = K // P
NODE_HALVES = 2
HALF = S // NODE_HALVES
OFFSETS_PER_COLUMN = 16
PIECE_COLUMNS = V // OFFSETS_PER_COLUMN

FLOPS = 2 * K * H * S + 2 * H * M * D * V

BF16, F32, U16 = mybir.dt.bfloat16, mybir.dt.float32, mybir.dt.uint16
TANH = mybir.ActivationFunctionType.Tanh


def tile_rows_gcn2_tanh_sum_kernel(tc, x, w, b, w2, offs, out):
    nc = tc.nc
    with (
        tc.tile_pool(name="sbuf", bufs=1) as sbuf,
        tc.psum_pool(name="psum", bufs=1) as psum,
    ):
        x_sb = sbuf.tile([P, K_BLOCKS, S], BF16)
        w_sb = sbuf.tile([P, K_BLOCKS, H], BF16)
        b_sb = sbuf.tile([H, 1], F32)
        w2_sb = sbuf.tile([H, M], BF16)
        offsets = sbuf.tile([P, D * PIECE_COLUMNS], U16)

        nc.sync.dma_start(x_sb[:], x.rearrange("(p a) s -> p a s", a=K_BLOCKS))
        nc.scalar.dma_start(w_sb[:], w.rearrange("(p a) h -> p a h", a=K_BLOCKS))
        nc.scalar.dma_start(b_sb[:], b)
        nc.sync.dma_start(w2_sb[:], w2)
        nc.sync.dma_start(offsets[:], offs)

        warm_in = sbuf.tile([P, 1], F32)
        warm_out = sbuf.tile([P, 1], F32)
        nc.vector.memset(warm_in[:], 0.0)
        nc.scalar.activation(warm_out[:], warm_in[:], TANH)

        h = sbuf.tile([H, S], BF16)
        for half in range(NODE_HALVES):
            nodes = slice(half * HALF, (half + 1) * HALF)
            pre = psum.tile([H, HALF], F32, name=f"pre{half}")
            for a in range(K_BLOCKS):
                nc.tensor.matmul(pre[:], w_sb[:, a, :], x_sb[:, a, nodes], start=(a == 0), stop=(a == K_BLOCKS - 1))
            nc.scalar.activation(h[:, nodes], pre[:], TANH, bias=b_sb[:])

        acc = psum.tile([M, V], F32)
        for t in range(D):
            piece = offsets[:, t * PIECE_COLUMNS : (t + 1) * PIECE_COLUMNS]
            nc.tensor.matmul(acc[:], w2_sb[:], h[:].indirect(piece), start=(t == 0), stop=(t == D - 1))

        out_sb = sbuf.tile([M, V], F32)
        nc.vector.tensor_copy(out_sb[:], acc[:])
        nc.sync.dma_start(out, out_sb[:])
